import numpy as np
import ml_dtypes


def mxq(x, axis, fmt="e4m3"):
    dtype, down = {"e4m3": (ml_dtypes.float8_e4m3fn, 7), "e5m2": (ml_dtypes.float8_e5m2, 14)}[fmt]
    v = np.moveaxis(np.asarray(x, np.float32).astype(ml_dtypes.bfloat16).astype(np.float64), axis, -1)
    blocks = v.reshape(v.shape[:-1] + (-1, 32))
    amax = np.abs(blocks).max(-1, keepdims=True)
    byte = np.maximum(np.where(amax > 0, np.frexp(amax)[1] - 1 + 127, 0) - down, 1)
    scale = np.exp2(byte - 127.0)
    codes = (blocks / scale).astype(np.float32).astype(dtype).astype(np.float64)
    return np.moveaxis((codes * scale).reshape(v.shape), -1, axis)


WIDE = False


def mx_kscale(k):
    if not WIDE:
        return np.ones(k)
    levels = np.array([10, -10, 5, -5, 0])
    if k % 512:
        return np.exp2(np.random.permutation(np.resize(levels, k // 32))).repeat(32)
    a = np.empty((k // 512, 16))
    for p in range(k // 512):
        a[p, :8] = np.random.permutation(np.resize(levels, 8))
        for g in range(8):
            far = levels[np.abs(levels - a[p, g]) >= 10]
            a[p, g + 8] = far[np.random.randint(len(far))]
    return np.exp2(a.ravel()).repeat(32)


BF16 = ml_dtypes.bfloat16


def bf(x):
    return np.asarray(x, np.float32).astype(BF16)


def f64(x):
    return np.asarray(x).astype(np.float64)


E2M1 = np.array([0.0, 0.5, 1.0, 1.5, 2.0, 3.0, 4.0, 6.0, -0.0, -0.5, -1.0, -1.5, -2.0, -3.0, -4.0, -6.0])


def pack_weight(w, fmt):
    k, n = w.shape
    w = f64(bf(w)).reshape(k // 32, 32, n)
    amax = np.abs(w).max(1)
    if fmt == "e4m3":
        byte = np.frexp(amax)[1] - 1 + 127 - 7
    else:
        mant, ex = np.frexp(amax / 6.0)
        byte = np.where(mant > 0.5, ex, ex - 1) + 127
    byte = np.clip(np.where(amax > 0, byte, 1), 1, 254)
    scaled = (w * np.exp2(127.0 - byte)[:, None, :]).reshape(k, n).astype(np.float32)
    by_word = np.ascontiguousarray(scaled.reshape(k // 512, 128, 4, n).transpose(0, 1, 3, 2))
    if fmt == "e4m3":
        words = by_word.astype(ml_dtypes.float8_e4m3fn).view(np.uint8)
    else:
        c = by_word.astype(ml_dtypes.float4_e2m1fn).view(np.uint8) & 0xF
        words = c[..., 0::2] | (c[..., 1::2] << 4)
    return np.ascontiguousarray(words), np.ascontiguousarray(byte.astype(np.uint8).reshape(k // 512, 16, n))


def unpack_weight(words, scales, fmt):
    g, p, n, _ = words.shape
    if fmt == "e4m3":
        vals = np.ascontiguousarray(words).view(ml_dtypes.float8_e4m3fn).astype(np.float64)
    else:
        nib = np.empty((g, p, n, 4), np.uint8)
        nib[..., 0::2] = words & 0xF
        nib[..., 1::2] = words >> 4
        vals = E2M1[nib]
    vals = vals * np.repeat(np.exp2(scales.astype(np.float64) - 127.0), 8, axis=1)[..., None]
    return vals.transpose(0, 1, 3, 2).reshape(g * 512, n)
def pack4(w):
    words, scales = pack_weight(w, "e2m1")
    return words.reshape(words.shape[0], 128, -1), scales


def unpack4(words, scales):
    return unpack_weight(words.reshape(words.shape[0], 128, -1, 2), scales, "e2m1")


E4M3FN = np.array([(-1.0 if i & 128 else 1.0) * ((1.0 + (i & 7) / 8.0) * 2.0 ** (((i >> 3) & 15) - 7) if i & 120 else (i & 7) * 2.0 ** -9) for i in range(256)])


def e4m3fn_bytes(y):
    return np.clip(np.asarray(y, np.float64), -448.0, 448.0).astype(np.float32).astype(ml_dtypes.float8_e4m3fn).view(np.uint8)


def e4m3fn_values(b):
    return E4M3FN[b]


B, D, F, O = 1024, 512, 1024, 512


def draw0():
    s, t = mx_kscale(D), mx_kscale(F)
    xb = bf(np.random.standard_normal((B, D)) * 0.8 * s)
    xg = bf(np.random.standard_normal((B, D)) * s)
    w1_words, w1_scales = pack4(np.random.standard_normal((D, F)) * 0.25 / np.sqrt(D) / s[:, None])
    b1 = bf(np.random.standard_normal(F) * 0.8)
    gain = bf((1.0 + 0.1 * np.random.standard_normal(F)) * t)
    w2_words, w2_scales = pack4(np.random.standard_normal((F, O)) * 2.0 / np.sqrt(F) / t[:, None])
    return {
        "xb": xb,
        "xg": xg,
        "w1_words": w1_words,
        "w1_scales": w1_scales,
        "b1": b1,
        "gain": gain,
        "w2_words": w2_words,
        "w2_scales": w2_scales,
    }


def split_bias(ub, ug, b1):
    share = (np.abs(ub) + 0.01) / (np.abs(ub) + np.abs(ug) + 0.02)
    pb = ub + share * b1
    pg = ug + (1.0 - share) * b1
    return pb, pg


def split_tanh(pb, pg):
    full = np.tanh(pb + pg)
    hb = 0.5 * (np.tanh(pb) + full - np.tanh(pg))
    hg = full - hb
    return hb, hg


def core(xb, xg, w1_words, w1_scales, b1, gain, w2_words, w2_scales):
    w1q = unpack4(w1_words, w1_scales)
    ub = mxq(f64(xb), 1, "e4m3") @ w1q
    ug = mxq(f64(xg), 1, "e4m3") @ w1q
    pb, pg = split_bias(ub, ug, f64(b1))
    hb, hg = split_tanh(pb, pg)
    w2q = unpack4(w2_words, w2_scales)
    g = f64(gain)
    yb = mxq(hb * g, 1, "e4m3") @ w2q
    yg = mxq(hg * g, 1, "e4m3") @ w2q
    return yb, yg


def setup_inputs():
    drawn = draw0()
    full = np.asarray(drawn['xg']).astype(np.float64)
    scale = (np.abs(full).reshape(8, 128, 4, 128).max(axis=(1, 3)) / 448.0).astype(np.float32)
    given = {}
    for key, value in drawn.items():
        if key == 'xg':
            given['xg_bytes'] = e4m3fn_bytes(full / np.repeat(np.repeat(scale.astype(np.float64), 128, axis=0), 128, axis=1))
            given['xg_scale'] = scale
        else:
            given[key] = value
    return given


def reference(xb, xg_bytes, xg_scale, w1_words, w1_scales, b1, gain, w2_words, w2_scales):
    return core(xb, e4m3fn_values(xg_bytes) * np.repeat(np.repeat(xg_scale.astype(np.float64), 128, axis=0), 128, axis=1), w1_words, w1_scales, b1, gain, w2_words, w2_scales)

@@ -1,0 +1,355 @@
+from contextlib import ExitStack
+
+import concourse.mybir as mybir
+from concourse.masks import make_identity
+
+B, D, F, O = 1024, 512, 1024, 512
+FLOPS = 4 * 2 * B * D * F
+
+F32 = mybir.dt.float32
+BF16 = mybir.dt.bfloat16
+I32 = mybir.dt.int32
+U32 = mybir.dt.uint32
+U8 = mybir.dt.uint8
+FP8 = mybir.dt.float8_e4m3fn
+FP8X4 = mybir.dt.float8_e4m3fn_x4
+FP4X4 = mybir.dt.float4_e2m1fn_x4
+AF = mybir.ActivationFunctionType
+ALU = mybir.AluOpType
+P = 128
+
+CHUNKS = (8, 8)
+LAG = 2
+GP_BLOCKS = (3, 7, 11, 12)
+Y_SCALAR = ((14, 1), (15, 1))
+
+
+def tile_contextualdecompositiontanhlayerpair_d2p_kernel(
+    tc, xb, xg_bytes, xg_scale, w1_words, w1_scales, b1, gain, w2_words, w2_scales, out_0, out_1
+):
+    nc = tc.nc
+    outs = (out_0, out_1)
+    with ExitStack() as ctx:
+        keep = ctx.enter_context(tc.tile_pool(name="keep", bufs=1))
+        work = ctx.enter_context(tc.tile_pool(name="work", bufs=2))
+        psum = ctx.enter_context(tc.psum_pool(name="psum", bufs=1))
+        ctx.enter_context(tc.manual_schedule(engines={mybir.EngineType.Activation}))
+
+        x_raw = []
+        x_byt = []
+        for q in range(4):
+            xr = keep.tile([P, 2, D], BF16, name=f"xr{q}", align_bytes=64)
+            xy = keep.tile([P, 2, D], U8, name=f"xbytes{q}", align_bytes=64)
+            x_raw.append(xr)
+            x_byt.append(xy)
+        w1_raw = keep.tile([P, 2 * F], U8, name="w1_raw", align_bytes=64)
+        w1s_raw = keep.tile([P, F], U8, name="w1s_raw", align_bytes=64)
+        w1_p = keep.tile([P, 2, 4, 256], U8, name="w1_p", align_bytes=64)
+        w1s_p = keep.tile([P, 2, 4, 128], U8, name="w1s_p", align_bytes=64)
+        w2_t = keep.tile([P, 2, 2 * O], U8, name="w2_t", align_bytes=64)
+        w2s_t = keep.tile([P, 2, O], U8, name="w2s_t", align_bytes=64)
+        sc_row = keep.tile([P, 32], F32, name="sc_row")
+        sc_col = keep.tile([P, 8], F32, name="sc_col")
+        b1_h = keep.tile([P, 8], BF16, name="b1_h")
+        g_h = keep.tile([P, 8], BF16, name="g_h")
+        b1_f = keep.tile([P, 8], F32, name="b1_f")
+        nb1_f = keep.tile([P, 8], F32, name="nb1_f")
+        g_f = keep.tile([P, 8], F32, name="g_f")
+        ident = keep.tile([P, P], F32, name="ident")
+        diag = keep.tile([P, 8, P], F32, name="diag")
+
+        nc.vector.memset(w1s_raw[:].bitcast(I32), 0)
+        nc.vector.memset(w2s_t[:].rearrange("p g n -> p (g n)").bitcast(I32), 0)
+        make_identity(nc, ident[:])
+
+        def load_x(q):
+            rows = slice(256 * q, 256 * q + 256)
+            nc.sync.dma_start(out=x_byt[q][:], in_=xg_bytes[rows, :].rearrange("(i p) k -> p i k", p=P))
+            nc.sync.dma_start(out=x_raw[q][:], in_=xb[rows, :].rearrange("(i p) k -> p i k", p=P))
+
+        load_x(0)
+        nc.sync.dma_start(out=w1_raw[:].bitcast(I32), in_=w1_words[0].bitcast(I32))
+        for quad in range(4):
+            nc.scalar.dma_start(
+                out=w1s_raw[32 * quad : 32 * quad + 4, :].bitcast(I32),
+                in_=w1_scales[0, 4 * quad : 4 * quad + 4, :].bitcast(I32),
+            )
+        nc.scalar.dma_start(out=sc_row[:], in_=xg_scale.rearrange("a b -> (a b)").partition_broadcast(P))
+        nc.scalar.dma_start(out=b1_h[:].rearrange("p (g t) -> p g t", t=4), in_=b1.rearrange("(g p t) -> p g t", p=P, t=4))
+        nc.scalar.dma_start(out=g_h[:].rearrange("p (g t) -> p g t", t=4), in_=gain.rearrange("(g p t) -> p g t", p=P, t=4))
+        for q in range(1, 4):
+            load_x(q)
+        nc.sync.dma_start(
+            out=w2_t[:].rearrange("p g n -> p (g n)").bitcast(I32).rearrange("p (g n) -> p g n", g=2),
+            in_=w2_words.bitcast(I32).rearrange("g p n -> p g n"),
+        )
+        for quad in range(4):
+            for g in range(2):
+                nc.sync.dma_start(
+                    out=w2s_t[32 * quad : 32 * quad + 4, g, :].bitcast(I32),
+                    in_=w2_scales[g, 4 * quad : 4 * quad + 4, :].bitcast(I32),
+                )
+
+        for j in range(4):
+            rows = slice(32 * j, 32 * j + 32)
+            nc.vector.tensor_copy(out=sc_col[rows, :], in_=sc_row[rows, :].rearrange("p (i j) -> p i j", j=4)[:, :, j])
+        nc.gpsimd.tensor_copy(out=b1_f[:], in_=b1_h[:])
+        nc.gpsimd.tensor_scalar(out=nb1_f[:], in0=b1_h[:], scalar1=-1.0, scalar2=0.0, op0=ALU.mult, op1=ALU.add)
+        nc.gpsimd.tensor_scalar(out=g_f[:], in0=g_h[:], scalar1=0.5, scalar2=0.0, op0=ALU.mult, op1=ALU.add)
+        for k in range(8):
+            nc.gpsimd.tensor_scalar(
+                out=diag[:, k, :], in0=ident[:], scalar1=g_f[:, k : k + 1], scalar2=0.0, op0=ALU.mult, op1=ALU.add
+            )
+        for g in range(2):
+            nc.vector.tensor_copy(
+                out=w1_p[:, g].rearrange("p t (m b) -> p t m b", b=2),
+                in_=w1_raw[:, 1024 * g : 1024 * g + 1024].rearrange("p (m t b) -> p t m b", t=4, b=2),
+            )
+            nc.vector.tensor_copy(
+                out=w1s_p[:, g], in_=w1s_raw[:, 512 * g : 512 * g + 512].rearrange("p (m t) -> p t m", t=4)
+            )
+
+        xb_c = keep.tile([P, 4, 256], U32, name="xb_c", align_bytes=64)
+        xb_s = keep.tile([P, 4, 256], U8, name="xb_s", align_bytes=64)
+        xg_c = keep.tile([P, 4, 256], U32, name="xg_c", align_bytes=64)
+        xg_s = keep.tile([P, 4, 256], U8, name="xg_s", align_bytes=64)
+
+        def transposes(bank, words):
+            for i in range(2):
+                for u in range(2):
+                    nc.tensor.transpose(bank[:, i, u, :], words[:, 256 * i + u : 256 * (i + 1) : 2], ident[:])
+
+        def xprep(q):
+            wide = work.tile([P, 2, D], BF16, name="wide", align_bytes=64)
+            nc.vector.tensor_copy(
+                out=wide[:].rearrange("p i k -> p (i k)"),
+                in_=x_byt[q][:].rearrange("p i k -> p (i k)").bitcast(FP8),
+            )
+            bankb = psum.tile([P, 2, 2, P], F32, name="bankb", tag="tu", bufs=2)
+            transposes(bankb, x_raw[q][:].rearrange("p i k -> p (i k)").bitcast(F32))
+            bankg = psum.tile([P, 2, 2, P], F32, name="bankg", tag="ts", bufs=2)
+            transposes(bankg, wide[:].rearrange("p i k -> p (i k)").bitcast(F32))
+            xbt = work.tile([P, 256, 4], BF16, name="xbt", align_bytes=64)
+            nc.scalar.copy(
+                out=xbt[:].rearrange("p n f -> p (n f)").bitcast(F32).rearrange("p (i n u) -> p i n u", i=2, u=2),
+                in_=bankb[:].rearrange("p i u n -> p i n u"),
+            )
+            xgt = work.tile([P, 256, 4], BF16, name="xgt", align_bytes=64)
+            bg = bankg[:].rearrange("p i u n -> p (i u n)").bitcast(BF16).rearrange("p (i u n e) -> p i n u e", i=2, u=2, e=2)
+            for i in range(2):
+                nc.vector.tensor_scalar(
+                    out=xgt[:, P * i : P * i + P, :].rearrange("p n (u e) -> p n u e", e=2),
+                    in0=bg[:, i],
+                    scalar1=sc_col[:, 2 * q + i : 2 * q + i + 1],
+                    scalar2=None,
+                    op0=ALU.mult,
+                )
+            nc.vector.quantize_mx(
+                out=xb_c[:, q, :].bitcast(FP8X4), scales=xb_s[:, q, :], in_=xbt[:].rearrange("p n f -> p (n f)")
+            )
+            nc.vector.quantize_mx(
+                out=xg_c[:, q, :].bitcast(FP8X4), scales=xg_s[:, q, :], in_=xgt[:].rearrange("p n f -> p (n f)")
+            )
+
+        def mx1(out, g, t, codes, scales, start, stop):
+            nc.tensor.matmul_mx(
+                out=out,
+                lhsT=w1_p[:, g, t, :].bitcast(FP4X4),
+                lhsT_scale=w1s_p[:, g, t, :],
+                rhs=codes.bitcast(FP8X4),
+                rhs_scale=scales,
+                start=start,
+                stop=stop,
+            )
+
+        st = {}
+
+        def idx(i):
+            return i // 4, (i // 2) % 2, i % 2
+
+        def magnitudes(i):
+            q, g, h = idx(i)
+            lb = psum.tile([P, 2, 256], F32, name="lb", tag="lb", bufs=1)
+            lg = psum.tile([P, 2, 256], F32, name="lg", tag="lg", bufs=1)
+            for t in range(2):
+                mx1(lb[:, t, :], g, 2 * h + t, xb_c[:, q, :], xb_s[:, q, :], True, True)
+            for t in range(2):
+                mx1(lg[:, t, :], g, 2 * h + t, xg_c[:, q, :], xg_s[:, q, :], True, True)
+            a = work.tile([P, 2, 256], F32, name="a", bufs=12)
+            c = work.tile([P, 2, 256], F32, name="c", bufs=4)
+            d = work.tile([P, 2, 256], F32, name="d", bufs=12)
+            nc.scalar.activation(out=a[:], in_=lb[:], func=AF.Abs)
+            nc.scalar.activation(out=c[:], in_=lg[:], func=AF.Abs)
+            nc.gpsimd.tensor_tensor(out=d[:], in0=a[:], in1=c[:], op=ALU.add)
+            st["a", i], st["d", i] = a, d
+
+        def log_sum(i):
+            d = st["d", i]
+            nc.scalar.activation(out=d[:], in_=d[:], func=AF.Ln, bias=0.02)
+
+        def split(i):
+            q, g, h = idx(i)
+            r = work.tile([P, 2, 256], F32, name="r", bufs=4)
+            nc.scalar.activation(out=r[:], in_=st["d", i][:], func=AF.Exp, scale=-1.0)
+            tu = psum.tile([P, 2, 256], F32, name="tu", tag="tu", bufs=2)
+            ts = psum.tile([P, 2, 256], F32, name="ts", tag="ts", bufs=2)
+            for t in range(2):
+                mx1(tu[:, t, :], g, 2 * h + t, xb_c[:, q, :], xb_s[:, q, :], True, True)
+            for t in range(2):
+                for m in range(2):
+                    cols = slice(P * m, P * m + P)
+                    mx1(ts[:, t, cols], g, 2 * h + t, xb_c[:, q, cols], xb_s[:, q, cols], True, False)
+                    mx1(ts[:, t, cols], g, 2 * h + t, xg_c[:, q, cols], xg_s[:, q, cols], False, True)
+            full = work.tile([P, 2, 256], F32, name="full", bufs=4)
+            if h == 0:
+                st["F", q, g] = work.tile([P, 4, 256], F32, name="fg", bufs=4)
+                st["tb", q, g] = work.tile([P, 4, 256], F32, name="tbg", bufs=4)
+                st["ng", q, g] = work.tile([P, 4, 256], F32, name="ngg", bufs=4)
+            fg = st["F", q, g]
+            for t in range(2):
+                k = 4 * g + 2 * h + t
+                nc.scalar.activation(out=full[:, t, :], in_=ts[:, t, :], func=AF.Tanh, bias=b1_f[:, k : k + 1])
+            sh = work.tile([P, 2, 256], F32, name="sh", bufs=4)
+            pb = work.tile([P, 2, 256], F32, name="pb", bufs=6)
+            w = work.tile([P, 2, 256], F32, name="w", bufs=6)
+            nc.vector.scalar_tensor_tensor(
+                out=sh[:], in0=st["a", i][:], scalar=0.01, in1=r[:], op0=ALU.add, op1=ALU.mult
+            )
+            for t in range(2):
+                k = 4 * g + 2 * h + t
+                nc.vector.scalar_tensor_tensor(
+                    out=pb[:, t, :], in0=sh[:, t, :], scalar=b1_f[:, k : k + 1], in1=tu[:, t, :], op0=ALU.mult, op1=ALU.add
+                )
+            nc.vector.tensor_tensor(out=w[:], in0=pb[:], in1=ts[:], op=ALU.subtract)
+            for t in range(2):
+                k = 4 * g + 2 * h + t
+                nc.vector.tensor_scalar(
+                    out=fg[:, 2 * h + t, :], in0=full[:, t, :], scalar1=g_f[:, k : k + 1], scalar2=None, op0=ALU.mult
+                )
+            st["pb", i], st["w", i] = pb, w
+
+        def tanhs(i):
+            q, g, h = idx(i)
+            tbg, ngg = st["tb", q, g], st["ng", q, g]
+            nc.scalar.activation(out=tbg[:, 2 * h : 2 * h + 2, :], in_=st["pb", i][:], func=AF.Tanh)
+            for t in range(2):
+                k = 4 * g + 2 * h + t
+                nc.scalar.activation(
+                    out=ngg[:, 2 * h + t, :], in_=st["w", i][:, t, :], func=AF.Tanh, bias=nb1_f[:, k : k + 1]
+                )
+
+        rot = {"d": ["d"], "y": ["y"]}
+
+        def bank_tag(kind):
+            tag = rot[kind].pop(0)
+            rot[kind].append(tag)
+            return tag
+
+        def block(k):
+            q, g, m = k // 4, (k // 2) % 2, k % 2
+            cols = slice(P * m, P * m + P)
+            fg, tbg, ngg = st["F", q, g], st["tb", q, g], st["ng", q, g]
+            if k in GP_BLOCKS:
+                dn = work.tile([P, 4, P], F32, name="dn", bufs=2)
+                dd = work.tile([P, 4, P], F32, name="dd", bufs=2)
+                nc.gpsimd.tensor_tensor(out=dn[:], in0=tbg[:, :, cols], in1=ngg[:, :, cols], op=ALU.add)
+                nc.gpsimd.tensor_tensor(
+                    out=dd[:],
+                    in0=dn[:],
+                    in1=g_f[:, 4 * g : 4 * g + 4].unsqueeze(2).to_broadcast([P, 4, P]),
+                    op=ALU.mult,
+                )
+            else:
+                tag = bank_tag("d")
+                dd = psum.tile([P, 4, P], F32, name="dd_" + tag, tag=tag, bufs=2 if tag in ("tu", "ts") else 1)
+                for t in range(4):
+                    nc.tensor.matmul(dd[:, t, :], lhsT=diag[:, 4 * g + t, :], rhs=tbg[:, t, cols], start=True, stop=False)
+                    nc.tensor.matmul(dd[:, t, :], lhsT=diag[:, 4 * g + t, :], rhs=ngg[:, t, cols], start=False, stop=True)
+            xy = work.tile([P, 2, P, 4], BF16, name="xy", bufs=4, align_bytes=64)
+            dv = dd[:].rearrange("p t (c i) -> p c t i", i=4)
+            fv = fg[:, :, cols].rearrange("p t (c i) -> p c t i", i=4)
+            nc.vector.tensor_tensor(
+                out=xy[:, 0].rearrange("p (c i) t -> p c t i", i=4), in0=fv, in1=dv, op=ALU.add
+            )
+            nc.vector.tensor_tensor(
+                out=xy[:, 1].rearrange("p (c i) t -> p c t i", i=4), in0=fv, in1=dv, op=ALU.subtract
+            )
+            hc = work.tile([P, 2, P], U32, name="hc", bufs=8, align_bytes=64)
+            hs = work.tile([P, 2, P], U8, name="hs", bufs=8, align_bytes=64)
+            nc.vector.quantize_mx(
+                out=hc[:].rearrange("p s n -> p (s n)").bitcast(FP8X4),
+                scales=hs[:].rearrange("p s n -> p (s n)"),
+                in_=xy[:].rearrange("p s n t -> p (s n t)"),
+            )
+            st["h", k] = (hc, hs)
+
+        def second(k):
+            q, m = k // 4, k % 2
+            for s in range(2):
+                tag = bank_tag("y")
+                yb = psum.tile([P, O], F32, name="y_" + tag, tag=tag, bufs=2 if tag in ("tu", "ts") else 1)
+                for g in range(2):
+                    hc, hs = st["h", k - 2 + 2 * g]
+                    nc.tensor.matmul_mx(
+                        out=yb[:],
+                        lhsT=hc[:, s, :].bitcast(FP8X4),
+                        lhsT_scale=hs[:, s, :],
+                        rhs=w2_t[:, g, :].bitcast(FP4X4),
+                        rhs_scale=w2s_t[:, g, :],
+                        start=(g == 0),
+                        stop=(g == 1),
+                    )
+                y = work.tile([P, O], F32, name="y", bufs=4)
+                if (k, s) in Y_SCALAR:
+                    nc.scalar.copy(out=y[:], in_=yb[:])
+                else:
+                    nc.vector.tensor_copy(out=y[:], in_=yb[:])
+                nc.sync.dma_start(out=outs[s][256 * q + P * m : 256 * q + P * m + P, :], in_=y[:])
+
+        bounds = [sum(CHUNKS[:j]) for j in range(len(CHUNKS) + 1)]
+        xprep(0)
+        for i in range(bounds[1]):
+            magnitudes(i)
+            if i < 3:
+                xprep(i + 1)
+        todo, ready = [], []
+        for j in range(len(CHUNKS)):
+            lo, hi = bounds[j], bounds[j + 1]
+            last = j == len(CHUNKS) - 1
+            if last:
+                rot["d"] = ["d", "lb", "lg"]
+            for i in range(lo, hi):
+                log_sum(i)
+            nxt = [] if last else list(range(hi, bounds[j + 2]))
+            steps = hi - lo + LAG
+            done = 0
+            for x in range(steps):
+                if lo + x < hi:
+                    split(lo + x)
+                want = (x + 1) * len(nxt) // steps
+                while done < want:
+                    magnitudes(nxt[done])
+                    done += 1
+                i = lo + x - LAG
+                if i >= lo:
+                    tanhs(i)
+                    if i % 2 == 1:
+                        todo.extend([i - 1, i])
+                if todo:
+                    k = todo.pop(0)
+                    block(k)
+                    if k % 4 >= 2:
+                        ready.append(k)
+                elif ready:
+                    second(ready.pop(0))
+                if len(ready) > 1:
+                    second(ready.pop(0))
+        rot["y"] = ["y", "tu", "ts"]
+        while todo or ready:
+            if todo:
+                k = todo.pop(0)
+                block(k)
+                if k % 4 >= 2:
+                    ready.append(k)
+            if ready and not todo:
+                second(ready.pop(0))

@@ -18,10 +18,17 @@ AF = mybir.ActivationFunctionType
 ALU = mybir.AluOpType
 P = 128
 
-CHUNKS = (8, 8)
+CHUNKS = (8, 8,)
 LAG = 2
-GP_BLOCKS = (3, 7, 11, 12)
-Y_SCALAR = ((14, 1), (15, 1))
+LEAD = 2
+AHEAD = 0
+YDEL = 3
+GP_BLOCKS = (5, 6, 13, 14,)
+Y_SCALAR = ((10, 0), (10, 1), (11, 0), (11, 1), (14, 0), (15, 0), (3, 0), (3, 1), (6, 0), (6, 1), (7, 1),)
+REC = (0,)
+RATIO = (14, 15,)
+SUM_V = (0, 1, 3, 4, 5, 6, 7, 8, 9, 10, 13, 14,)
+CB = 10
 
 
 def tile_contextualdecompositiontanhlayerpair_d2p_kernel(
@@ -54,6 +61,8 @@ def tile_contextualdecompositiontanhlayerpair_d2p_kernel(
         g_h = keep.tile([P, 8], BF16, name="g_h")
         b1_f = keep.tile([P, 8], F32, name="b1_f")
         nb1_f = keep.tile([P, 8], F32, name="nb1_f")
+        hb1_f = keep.tile([P, 8], F32, name="hb1_f")
+        nhb1_f = keep.tile([P, 8], F32, name="nhb1_f")
         g_f = keep.tile([P, 8], F32, name="g_f")
         ident = keep.tile([P, P], F32, name="ident")
         diag = keep.tile([P, 8, P], F32, name="diag")
@@ -95,6 +104,8 @@ def tile_contextualdecompositiontanhlayerpair_d2p_kernel(
             nc.vector.tensor_copy(out=sc_col[rows, :], in_=sc_row[rows, :].rearrange("p (i j) -> p i j", j=4)[:, :, j])
         nc.gpsimd.tensor_copy(out=b1_f[:], in_=b1_h[:])
         nc.gpsimd.tensor_scalar(out=nb1_f[:], in0=b1_h[:], scalar1=-1.0, scalar2=0.0, op0=ALU.mult, op1=ALU.add)
+        nc.gpsimd.tensor_scalar(out=hb1_f[:], in0=b1_h[:], scalar1=0.5, scalar2=0.0, op0=ALU.mult, op1=ALU.add)
+        nc.gpsimd.tensor_scalar(out=nhb1_f[:], in0=b1_h[:], scalar1=-0.5, scalar2=0.0, op0=ALU.mult, op1=ALU.add)
         nc.gpsimd.tensor_scalar(out=g_f[:], in0=g_h[:], scalar1=0.5, scalar2=0.0, op0=ALU.mult, op1=ALU.add)
         for k in range(8):
             nc.gpsimd.tensor_scalar(
@@ -167,7 +178,7 @@ def tile_contextualdecompositiontanhlayerpair_d2p_kernel(
         def idx(i):
             return i // 4, (i // 2) % 2, i % 2
 
-        def magnitudes(i):
+        def magnitudes_mm(i):
             q, g, h = idx(i)
             lb = psum.tile([P, 2, 256], F32, name="lb", tag="lb", bufs=1)
             lg = psum.tile([P, 2, 256], F32, name="lg", tag="lg", bufs=1)
@@ -175,22 +186,56 @@ def tile_contextualdecompositiontanhlayerpair_d2p_kernel(
                 mx1(lb[:, t, :], g, 2 * h + t, xb_c[:, q, :], xb_s[:, q, :], True, True)
             for t in range(2):
                 mx1(lg[:, t, :], g, 2 * h + t, xg_c[:, q, :], xg_s[:, q, :], True, True)
+            st["lb", i], st["lg", i] = lb, lg
+
+        def magnitudes(i):
+            lb, lg = st["lb", i], st["lg", i]
             a = work.tile([P, 2, 256], F32, name="a", bufs=12)
-            c = work.tile([P, 2, 256], F32, name="c", bufs=4)
-            d = work.tile([P, 2, 256], F32, name="d", bufs=12)
+            c = work.tile([P, 2, 256], F32, name="c", bufs=CB)
             nc.scalar.activation(out=a[:], in_=lb[:], func=AF.Abs)
             nc.scalar.activation(out=c[:], in_=lg[:], func=AF.Abs)
-            nc.gpsimd.tensor_tensor(out=d[:], in0=a[:], in1=c[:], op=ALU.add)
-            st["a", i], st["d", i] = a, d
+            st["a", i], st["c", i] = a, c
+            if i in REC:
+                d = work.tile([P, 2, 256], F32, name="d", bufs=12)
+                nc.vector.scalar_tensor_tensor(out=d[:], in0=a[:], scalar=0.02, in1=c[:], op0=ALU.add, op1=ALU.add)
+                st["d", i] = d
+                if len(REC) == 1:
+                    r = work.tile([P, 2, 256], F32, name="r", bufs=4)
+                    nc.vector.reciprocal(out=r[:], in_=d[:])
+                    st["r", i] = r
+                elif i == REC[1]:
+                    pr = work.tile([P, 2, 256], F32, name="pr", bufs=1)
+                    ir = work.tile([P, 2, 256], F32, name="ir", bufs=1)
+                    d0 = st["d", REC[0]]
+                    nc.vector.tensor_tensor(out=pr[:], in0=d0[:], in1=d[:], op=ALU.mult)
+                    nc.vector.reciprocal(out=ir[:], in_=pr[:])
+                    for n, other in ((REC[0], d), (REC[1], d0)):
+                        r = work.tile([P, 2, 256], F32, name="r", bufs=4)
+                        nc.vector.tensor_tensor(out=r[:], in0=ir[:], in1=other[:], op=ALU.mult)
+                        st["r", n] = r
+            elif i not in RATIO:
+                d = work.tile([P, 2, 256], F32, name="d", bufs=12)
+                eng = nc.vector if i in SUM_V else nc.gpsimd
+                eng.tensor_tensor(out=d[:], in0=a[:], in1=c[:], op=ALU.add)
+                st["d", i] = d
 
         def log_sum(i):
+            if i in REC:
+                return
+            if i in RATIO:
+                a, c = st["a", i], st["c", i]
+                nc.scalar.activation(out=a[:], in_=a[:], func=AF.Ln, bias=0.01)
+                nc.scalar.activation(out=c[:], in_=c[:], func=AF.Ln, bias=0.01)
+                d = work.tile([P, 2, 256], F32, name="d", bufs=12)
+                eng = nc.vector if i in SUM_V else nc.gpsimd
+                eng.tensor_tensor(out=d[:], in0=a[:], in1=c[:], op=ALU.subtract)
+                st["d", i] = d
+                return
             d = st["d", i]
             nc.scalar.activation(out=d[:], in_=d[:], func=AF.Ln, bias=0.02)
 
-        def split(i):
+        def split_mm(i):
             q, g, h = idx(i)
-            r = work.tile([P, 2, 256], F32, name="r", bufs=4)
-            nc.scalar.activation(out=r[:], in_=st["d", i][:], func=AF.Exp, scale=-1.0)
             tu = psum.tile([P, 2, 256], F32, name="tu", tag="tu", bufs=2)
             ts = psum.tile([P, 2, 256], F32, name="ts", tag="ts", bufs=2)
             for t in range(2):
@@ -200,25 +245,41 @@ def tile_contextualdecompositiontanhlayerpair_d2p_kernel(
                     cols = slice(P * m, P * m + P)
                     mx1(ts[:, t, cols], g, 2 * h + t, xb_c[:, q, cols], xb_s[:, q, cols], True, False)
                     mx1(ts[:, t, cols], g, 2 * h + t, xg_c[:, q, cols], xg_s[:, q, cols], False, True)
+            st["tu", i], st["ts", i] = tu, ts
+
+        def split(i):
+            q, g, h = idx(i)
+            tu, ts = st["tu", i], st["ts", i]
+            if i in REC:
+                r = st["r", i]
+            else:
+                r = work.tile([P, 2, 256], F32, name="r", bufs=4)
+                if i in RATIO:
+                    nc.scalar.activation(out=r[:], in_=st["d", i][:], func=AF.Tanh, scale=0.5)
+                else:
+                    nc.scalar.activation(out=r[:], in_=st["d", i][:], func=AF.Exp, scale=-1.0)
             full = work.tile([P, 2, 256], F32, name="full", bufs=4)
             if h == 0:
-                st["F", q, g] = work.tile([P, 4, 256], F32, name="fg", bufs=4)
-                st["tb", q, g] = work.tile([P, 4, 256], F32, name="tbg", bufs=4)
-                st["ng", q, g] = work.tile([P, 4, 256], F32, name="ngg", bufs=4)
+                st["F", q, g] = work.tile([P, 4, 256], F32, name="fg", bufs=3)
+                st["tb", q, g] = work.tile([P, 4, 256], F32, name="tbg", bufs=3)
+                st["ng", q, g] = work.tile([P, 4, 256], F32, name="ngg", bufs=3)
             fg = st["F", q, g]
             for t in range(2):
                 k = 4 * g + 2 * h + t
                 nc.scalar.activation(out=full[:, t, :], in_=ts[:, t, :], func=AF.Tanh, bias=b1_f[:, k : k + 1])
-            sh = work.tile([P, 2, 256], F32, name="sh", bufs=4)
-            pb = work.tile([P, 2, 256], F32, name="pb", bufs=6)
-            w = work.tile([P, 2, 256], F32, name="w", bufs=6)
-            nc.vector.scalar_tensor_tensor(
-                out=sh[:], in0=st["a", i][:], scalar=0.01, in1=r[:], op0=ALU.add, op1=ALU.mult
-            )
+            pb = work.tile([P, 2, 256], F32, name="pb", bufs=4)
+            w = work.tile([P, 2, 256], F32, name="w", bufs=4)
+            if i in RATIO:
+                sh, scal = r, hb1_f
+            else:
+                sh, scal = work.tile([P, 2, 256], F32, name="sh", bufs=4), b1_f
+                nc.vector.scalar_tensor_tensor(
+                    out=sh[:], in0=st["a", i][:], scalar=0.01, in1=r[:], op0=ALU.add, op1=ALU.mult
+                )
             for t in range(2):
                 k = 4 * g + 2 * h + t
                 nc.vector.scalar_tensor_tensor(
-                    out=pb[:, t, :], in0=sh[:, t, :], scalar=b1_f[:, k : k + 1], in1=tu[:, t, :], op0=ALU.mult, op1=ALU.add
+                    out=pb[:, t, :], in0=sh[:, t, :], scalar=scal[:, k : k + 1], in1=tu[:, t, :], op0=ALU.mult, op1=ALU.add
                 )
             nc.vector.tensor_tensor(out=w[:], in0=pb[:], in1=ts[:], op=ALU.subtract)
             for t in range(2):
@@ -231,11 +292,19 @@ def tile_contextualdecompositiontanhlayerpair_d2p_kernel(
         def tanhs(i):
             q, g, h = idx(i)
             tbg, ngg = st["tb", q, g], st["ng", q, g]
-            nc.scalar.activation(out=tbg[:, 2 * h : 2 * h + 2, :], in_=st["pb", i][:], func=AF.Tanh)
+            nb = nhb1_f if i in RATIO else nb1_f
+            if i in RATIO:
+                for t in range(2):
+                    k = 4 * g + 2 * h + t
+                    nc.scalar.activation(
+                        out=tbg[:, 2 * h + t, :], in_=st["pb", i][:, t, :], func=AF.Tanh, bias=hb1_f[:, k : k + 1]
+                    )
+            else:
+                nc.scalar.activation(out=tbg[:, 2 * h : 2 * h + 2, :], in_=st["pb", i][:], func=AF.Tanh)
             for t in range(2):
                 k = 4 * g + 2 * h + t
                 nc.scalar.activation(
-                    out=ngg[:, 2 * h + t, :], in_=st["w", i][:, t, :], func=AF.Tanh, bias=nb1_f[:, k : k + 1]
+                    out=ngg[:, 2 * h + t, :], in_=st["w", i][:, t, :], func=AF.Tanh, bias=nb[:, k : k + 1]
                 )
 
         rot = {"d": ["d"], "y": ["y"]}
@@ -283,41 +352,68 @@ def tile_contextualdecompositiontanhlayerpair_d2p_kernel(
             )
             st["h", k] = (hc, hs)
 
-        def second(k):
+        def second(k, s):
+            tag = bank_tag("y")
+            yb = psum.tile([P, O], F32, name="y_" + tag, tag=tag, bufs=2 if tag in ("tu", "ts") else 1)
+            for g in range(2):
+                hc, hs = st["h", k - 2 + 2 * g]
+                nc.tensor.matmul_mx(
+                    out=yb[:],
+                    lhsT=hc[:, s, :].bitcast(FP8X4),
+                    lhsT_scale=hs[:, s, :],
+                    rhs=w2_t[:, g, :].bitcast(FP4X4),
+                    rhs_scale=w2s_t[:, g, :],
+                    start=(g == 0),
+                    stop=(g == 1),
+                )
+            st["y", k, s] = yb
+
+        def second_out(k, s):
             q, m = k // 4, k % 2
-            for s in range(2):
-                tag = bank_tag("y")
-                yb = psum.tile([P, O], F32, name="y_" + tag, tag=tag, bufs=2 if tag in ("tu", "ts") else 1)
-                for g in range(2):
-                    hc, hs = st["h", k - 2 + 2 * g]
-                    nc.tensor.matmul_mx(
-                        out=yb[:],
-                        lhsT=hc[:, s, :].bitcast(FP8X4),
-                        lhsT_scale=hs[:, s, :],
-                        rhs=w2_t[:, g, :].bitcast(FP4X4),
-                        rhs_scale=w2s_t[:, g, :],
-                        start=(g == 0),
-                        stop=(g == 1),
-                    )
-                y = work.tile([P, O], F32, name="y", bufs=4)
-                if (k, s) in Y_SCALAR:
-                    nc.scalar.copy(out=y[:], in_=yb[:])
-                else:
-                    nc.vector.tensor_copy(out=y[:], in_=yb[:])
-                nc.sync.dma_start(out=outs[s][256 * q + P * m : 256 * q + P * m + P, :], in_=y[:])
+            yb = st["y", k, s]
+            y = work.tile([P, O], F32, name="y", bufs=4)
+            if (k, s) in Y_SCALAR:
+                nc.scalar.copy(out=y[:], in_=yb[:])
+            else:
+                nc.vector.tensor_copy(out=y[:], in_=yb[:])
+            nc.sync.dma_start(out=outs[s][256 * q + P * m : 256 * q + P * m + P, :], in_=y[:])
 
         bounds = [sum(CHUNKS[:j]) for j in range(len(CHUNKS) + 1)]
+        seen_l, seen_t = set(), set()
+
+        def mm_l(i):
+            if i < 16 and i not in seen_l:
+                seen_l.add(i)
+                magnitudes_mm(i)
+
+        def mm_t(i):
+            if i < 16 and i not in seen_t:
+                seen_t.add(i)
+                split_mm(i)
+
         xprep(0)
         for i in range(bounds[1]):
+            mm_l(i)
             magnitudes(i)
+            mm_l(i + 1) if i + 1 < 4 else None
             if i < 3:
                 xprep(i + 1)
-        todo, ready = [], []
+        todo, ready, late = [], [], []
+
+        def step_block():
+            k = todo.pop(0)
+            block(k)
+            if k % 4 >= 2:
+                ready.extend([(k, 0), (k, 1)])
+
         for j in range(len(CHUNKS)):
             lo, hi = bounds[j], bounds[j + 1]
             last = j == len(CHUNKS) - 1
             if last:
-                rot["d"] = ["d", "lb", "lg"]
+                rot["d"] = ["d", "lb"]
+                rot["y"] = ["y", "lg"]
+            for i in range(lo, min(hi, lo + LEAD)):
+                mm_t(i)
             for i in range(lo, hi):
                 log_sum(i)
             nxt = [] if last else list(range(hi, bounds[j + 2]))
@@ -325,31 +421,40 @@ def tile_contextualdecompositiontanhlayerpair_d2p_kernel(
             done = 0
             for x in range(steps):
                 if lo + x < hi:
+                    mm_t(lo + x)
                     split(lo + x)
-                want = (x + 1) * len(nxt) // steps
+                for i in range(lo + x, min(hi, lo + x + 1 + LEAD)):
+                    mm_t(i)
+                want = min(len(nxt), -((-(x + 1) * len(nxt)) // max(1, steps - AHEAD)))
                 while done < want:
+                    mm_l(nxt[done])
                     magnitudes(nxt[done])
                     done += 1
+                    if LEAD and done < len(nxt):
+                        mm_l(nxt[done])
                 i = lo + x - LAG
                 if i >= lo:
                     tanhs(i)
                     if i % 2 == 1:
                         todo.extend([i - 1, i])
+                while late and late[0][0] <= 0:
+                    second_out(*late.pop(0)[1])
+                late = [(age - 1, ks) for age, ks in late]
                 if todo:
-                    k = todo.pop(0)
-                    block(k)
-                    if k % 4 >= 2:
-                        ready.append(k)
-                elif ready:
-                    second(ready.pop(0))
-                if len(ready) > 1:
-                    second(ready.pop(0))
-        rot["y"] = ["y", "tu", "ts"]
+                    step_block()
+                for n in range(2 if len(ready) > 2 or not todo else 1):
+                    if ready:
+                        ks = ready.pop(0)
+                        second(*ks)
+                        late.append((YDEL if ks in Y_SCALAR else 0, ks))
+        while late:
+            second_out(*late.pop(0)[1])
+        rot["y"] = ["y", "lg", "tu", "ts"]
+        rot["d"] = ["d", "lb"]
         while todo or ready:
-            if todo:
-                k = todo.pop(0)
-                block(k)
-                if k % 4 >= 2:
-                    ready.append(k)
-            if ready and not todo:
-                second(ready.pop(0))
+            while todo:
+                step_block()
+            while ready:
+                ks = ready.pop(0)
+                second(*ks)
+                second_out(*ks)

from contextlib import ExitStack

import concourse.mybir as mybir
from concourse.masks import make_identity

B, D, F, O = 1024, 512, 1024, 512
FLOPS = 4 * 2 * B * D * F

F32 = mybir.dt.float32
BF16 = mybir.dt.bfloat16
I32 = mybir.dt.int32
U32 = mybir.dt.uint32
U8 = mybir.dt.uint8
FP8 = mybir.dt.float8_e4m3fn
FP8X4 = mybir.dt.float8_e4m3fn_x4
FP4X4 = mybir.dt.float4_e2m1fn_x4
AF = mybir.ActivationFunctionType
ALU = mybir.AluOpType
P = 128

CHUNKS = (8, 8,)
LAG = 2
LEAD = 2
AHEAD = 0
YDEL = 3
GP_BLOCKS = (5, 6, 13, 14,)
Y_SCALAR = ((10, 0), (10, 1), (11, 0), (11, 1), (14, 0), (15, 0), (3, 0), (3, 1), (6, 0), (6, 1), (7, 1),)
REC = (0,)
RATIO = (14, 15,)
SUM_V = (0, 1, 3, 4, 5, 6, 7, 8, 9, 10, 13, 14,)
CB = 10


def tile_contextualdecompositiontanhlayerpair_d2p_kernel(
    tc, xb, xg_bytes, xg_scale, w1_words, w1_scales, b1, gain, w2_words, w2_scales, out_0, out_1
):
    nc = tc.nc
    outs = (out_0, out_1)
    with ExitStack() as ctx:
        keep = ctx.enter_context(tc.tile_pool(name="keep", bufs=1))
        work = ctx.enter_context(tc.tile_pool(name="work", bufs=2))
        psum = ctx.enter_context(tc.psum_pool(name="psum", bufs=1))
        ctx.enter_context(tc.manual_schedule(engines={mybir.EngineType.Activation}))

        x_raw = []
        x_byt = []
        for q in range(4):
            xr = keep.tile([P, 2, D], BF16, name=f"xr{q}", align_bytes=64)
            xy = keep.tile([P, 2, D], U8, name=f"xbytes{q}", align_bytes=64)
            x_raw.append(xr)
            x_byt.append(xy)
        w1_raw = keep.tile([P, 2 * F], U8, name="w1_raw", align_bytes=64)
        w1s_raw = keep.tile([P, F], U8, name="w1s_raw", align_bytes=64)
        w1_p = keep.tile([P, 2, 4, 256], U8, name="w1_p", align_bytes=64)
        w1s_p = keep.tile([P, 2, 4, 128], U8, name="w1s_p", align_bytes=64)
        w2_t = keep.tile([P, 2, 2 * O], U8, name="w2_t", align_bytes=64)
        w2s_t = keep.tile([P, 2, O], U8, name="w2s_t", align_bytes=64)
        sc_row = keep.tile([P, 32], F32, name="sc_row")
        sc_col = keep.tile([P, 8], F32, name="sc_col")
        b1_h = keep.tile([P, 8], BF16, name="b1_h")
        g_h = keep.tile([P, 8], BF16, name="g_h")
        b1_f = keep.tile([P, 8], F32, name="b1_f")
        nb1_f = keep.tile([P, 8], F32, name="nb1_f")
        hb1_f = keep.tile([P, 8], F32, name="hb1_f")
        nhb1_f = keep.tile([P, 8], F32, name="nhb1_f")
        g_f = keep.tile([P, 8], F32, name="g_f")
        ident = keep.tile([P, P], F32, name="ident")
        diag = keep.tile([P, 8, P], F32, name="diag")

        nc.vector.memset(w1s_raw[:].bitcast(I32), 0)
        nc.vector.memset(w2s_t[:].rearrange("p g n -> p (g n)").bitcast(I32), 0)
        make_identity(nc, ident[:])

        def load_x(q):
            rows = slice(256 * q, 256 * q + 256)
            nc.sync.dma_start(out=x_byt[q][:], in_=xg_bytes[rows, :].rearrange("(i p) k -> p i k", p=P))
            nc.sync.dma_start(out=x_raw[q][:], in_=xb[rows, :].rearrange("(i p) k -> p i k", p=P))

        load_x(0)
        nc.sync.dma_start(out=w1_raw[:].bitcast(I32), in_=w1_words[0].bitcast(I32))
        for quad in range(4):
            nc.scalar.dma_start(
                out=w1s_raw[32 * quad : 32 * quad + 4, :].bitcast(I32),
                in_=w1_scales[0, 4 * quad : 4 * quad + 4, :].bitcast(I32),
            )
        nc.scalar.dma_start(out=sc_row[:], in_=xg_scale.rearrange("a b -> (a b)").partition_broadcast(P))
        nc.scalar.dma_start(out=b1_h[:].rearrange("p (g t) -> p g t", t=4), in_=b1.rearrange("(g p t) -> p g t", p=P, t=4))
        nc.scalar.dma_start(out=g_h[:].rearrange("p (g t) -> p g t", t=4), in_=gain.rearrange("(g p t) -> p g t", p=P, t=4))
        for q in range(1, 4):
            load_x(q)
        nc.sync.dma_start(
            out=w2_t[:].rearrange("p g n -> p (g n)").bitcast(I32).rearrange("p (g n) -> p g n", g=2),
            in_=w2_words.bitcast(I32).rearrange("g p n -> p g n"),
        )
        for quad in range(4):
            for g in range(2):
                nc.sync.dma_start(
                    out=w2s_t[32 * quad : 32 * quad + 4, g, :].bitcast(I32),
                    in_=w2_scales[g, 4 * quad : 4 * quad + 4, :].bitcast(I32),
                )

        for j in range(4):
            rows = slice(32 * j, 32 * j + 32)
            nc.vector.tensor_copy(out=sc_col[rows, :], in_=sc_row[rows, :].rearrange("p (i j) -> p i j", j=4)[:, :, j])
        nc.gpsimd.tensor_copy(out=b1_f[:], in_=b1_h[:])
        nc.gpsimd.tensor_scalar(out=nb1_f[:], in0=b1_h[:], scalar1=-1.0, scalar2=0.0, op0=ALU.mult, op1=ALU.add)
        nc.gpsimd.tensor_scalar(out=hb1_f[:], in0=b1_h[:], scalar1=0.5, scalar2=0.0, op0=ALU.mult, op1=ALU.add)
        nc.gpsimd.tensor_scalar(out=nhb1_f[:], in0=b1_h[:], scalar1=-0.5, scalar2=0.0, op0=ALU.mult, op1=ALU.add)
        nc.gpsimd.tensor_scalar(out=g_f[:], in0=g_h[:], scalar1=0.5, scalar2=0.0, op0=ALU.mult, op1=ALU.add)
        for k in range(8):
            nc.gpsimd.tensor_scalar(
                out=diag[:, k, :], in0=ident[:], scalar1=g_f[:, k : k + 1], scalar2=0.0, op0=ALU.mult, op1=ALU.add
            )
        for g in range(2):
            nc.vector.tensor_copy(
                out=w1_p[:, g].rearrange("p t (m b) -> p t m b", b=2),
                in_=w1_raw[:, 1024 * g : 1024 * g + 1024].rearrange("p (m t b) -> p t m b", t=4, b=2),
            )
            nc.vector.tensor_copy(
                out=w1s_p[:, g], in_=w1s_raw[:, 512 * g : 512 * g + 512].rearrange("p (m t) -> p t m", t=4)
            )

        xb_c = keep.tile([P, 4, 256], U32, name="xb_c", align_bytes=64)
        xb_s = keep.tile([P, 4, 256], U8, name="xb_s", align_bytes=64)
        xg_c = keep.tile([P, 4, 256], U32, name="xg_c", align_bytes=64)
        xg_s = keep.tile([P, 4, 256], U8, name="xg_s", align_bytes=64)

        def transposes(bank, words):
            for i in range(2):
                for u in range(2):
                    nc.tensor.transpose(bank[:, i, u, :], words[:, 256 * i + u : 256 * (i + 1) : 2], ident[:])

        def xprep(q):
            wide = work.tile([P, 2, D], BF16, name="wide", align_bytes=64)
            nc.vector.tensor_copy(
                out=wide[:].rearrange("p i k -> p (i k)"),
                in_=x_byt[q][:].rearrange("p i k -> p (i k)").bitcast(FP8),
            )
            bankb = psum.tile([P, 2, 2, P], F32, name="bankb", tag="tu", bufs=2)
            transposes(bankb, x_raw[q][:].rearrange("p i k -> p (i k)").bitcast(F32))
            bankg = psum.tile([P, 2, 2, P], F32, name="bankg", tag="ts", bufs=2)
            transposes(bankg, wide[:].rearrange("p i k -> p (i k)").bitcast(F32))
            xbt = work.tile([P, 256, 4], BF16, name="xbt", align_bytes=64)
            nc.scalar.copy(
                out=xbt[:].rearrange("p n f -> p (n f)").bitcast(F32).rearrange("p (i n u) -> p i n u", i=2, u=2),
                in_=bankb[:].rearrange("p i u n -> p i n u"),
            )
            xgt = work.tile([P, 256, 4], BF16, name="xgt", align_bytes=64)
            bg = bankg[:].rearrange("p i u n -> p (i u n)").bitcast(BF16).rearrange("p (i u n e) -> p i n u e", i=2, u=2, e=2)
            for i in range(2):
                nc.vector.tensor_scalar(
                    out=xgt[:, P * i : P * i + P, :].rearrange("p n (u e) -> p n u e", e=2),
                    in0=bg[:, i],
                    scalar1=sc_col[:, 2 * q + i : 2 * q + i + 1],
                    scalar2=None,
                    op0=ALU.mult,
                )
            nc.vector.quantize_mx(
                out=xb_c[:, q, :].bitcast(FP8X4), scales=xb_s[:, q, :], in_=xbt[:].rearrange("p n f -> p (n f)")
            )
            nc.vector.quantize_mx(
                out=xg_c[:, q, :].bitcast(FP8X4), scales=xg_s[:, q, :], in_=xgt[:].rearrange("p n f -> p (n f)")
            )

        def mx1(out, g, t, codes, scales, start, stop):
            nc.tensor.matmul_mx(
                out=out,
                lhsT=w1_p[:, g, t, :].bitcast(FP4X4),
                lhsT_scale=w1s_p[:, g, t, :],
                rhs=codes.bitcast(FP8X4),
                rhs_scale=scales,
                start=start,
                stop=stop,
            )

        st = {}

        def idx(i):
            return i // 4, (i // 2) % 2, i % 2

        def magnitudes_mm(i):
            q, g, h = idx(i)
            lb = psum.tile([P, 2, 256], F32, name="lb", tag="lb", bufs=1)
            lg = psum.tile([P, 2, 256], F32, name="lg", tag="lg", bufs=1)
            for t in range(2):
                mx1(lb[:, t, :], g, 2 * h + t, xb_c[:, q, :], xb_s[:, q, :], True, True)
            for t in range(2):
                mx1(lg[:, t, :], g, 2 * h + t, xg_c[:, q, :], xg_s[:, q, :], True, True)
            st["lb", i], st["lg", i] = lb, lg

        def magnitudes(i):
            lb, lg = st["lb", i], st["lg", i]
            a = work.tile([P, 2, 256], F32, name="a", bufs=12)
            c = work.tile([P, 2, 256], F32, name="c", bufs=CB)
            nc.scalar.activation(out=a[:], in_=lb[:], func=AF.Abs)
            nc.scalar.activation(out=c[:], in_=lg[:], func=AF.Abs)
            st["a", i], st["c", i] = a, c
            if i in REC:
                d = work.tile([P, 2, 256], F32, name="d", bufs=12)
                nc.vector.scalar_tensor_tensor(out=d[:], in0=a[:], scalar=0.02, in1=c[:], op0=ALU.add, op1=ALU.add)
                st["d", i] = d
                if len(REC) == 1:
                    r = work.tile([P, 2, 256], F32, name="r", bufs=4)
                    nc.vector.reciprocal(out=r[:], in_=d[:])
                    st["r", i] = r
                elif i == REC[1]:
                    pr = work.tile([P, 2, 256], F32, name="pr", bufs=1)
                    ir = work.tile([P, 2, 256], F32, name="ir", bufs=1)
                    d0 = st["d", REC[0]]
                    nc.vector.tensor_tensor(out=pr[:], in0=d0[:], in1=d[:], op=ALU.mult)
                    nc.vector.reciprocal(out=ir[:], in_=pr[:])
                    for n, other in ((REC[0], d), (REC[1], d0)):
                        r = work.tile([P, 2, 256], F32, name="r", bufs=4)
                        nc.vector.tensor_tensor(out=r[:], in0=ir[:], in1=other[:], op=ALU.mult)
                        st["r", n] = r
            elif i not in RATIO:
                d = work.tile([P, 2, 256], F32, name="d", bufs=12)
                eng = nc.vector if i in SUM_V else nc.gpsimd
                eng.tensor_tensor(out=d[:], in0=a[:], in1=c[:], op=ALU.add)
                st["d", i] = d

        def log_sum(i):
            if i in REC:
                return
            if i in RATIO:
                a, c = st["a", i], st["c", i]
                nc.scalar.activation(out=a[:], in_=a[:], func=AF.Ln, bias=0.01)
                nc.scalar.activation(out=c[:], in_=c[:], func=AF.Ln, bias=0.01)
                d = work.tile([P, 2, 256], F32, name="d", bufs=12)
                eng = nc.vector if i in SUM_V else nc.gpsimd
                eng.tensor_tensor(out=d[:], in0=a[:], in1=c[:], op=ALU.subtract)
                st["d", i] = d
                return
            d = st["d", i]
            nc.scalar.activation(out=d[:], in_=d[:], func=AF.Ln, bias=0.02)

        def split_mm(i):
            q, g, h = idx(i)
            tu = psum.tile([P, 2, 256], F32, name="tu", tag="tu", bufs=2)
            ts = psum.tile([P, 2, 256], F32, name="ts", tag="ts", bufs=2)
            for t in range(2):
                mx1(tu[:, t, :], g, 2 * h + t, xb_c[:, q, :], xb_s[:, q, :], True, True)
            for t in range(2):
                for m in range(2):
                    cols = slice(P * m, P * m + P)
                    mx1(ts[:, t, cols], g, 2 * h + t, xb_c[:, q, cols], xb_s[:, q, cols], True, False)
                    mx1(ts[:, t, cols], g, 2 * h + t, xg_c[:, q, cols], xg_s[:, q, cols], False, True)
            st["tu", i], st["ts", i] = tu, ts

        def split(i):
            q, g, h = idx(i)
            tu, ts = st["tu", i], st["ts", i]
            if i in REC:
                r = st["r", i]
            else:
                r = work.tile([P, 2, 256], F32, name="r", bufs=4)
                if i in RATIO:
                    nc.scalar.activation(out=r[:], in_=st["d", i][:], func=AF.Tanh, scale=0.5)
                else:
                    nc.scalar.activation(out=r[:], in_=st["d", i][:], func=AF.Exp, scale=-1.0)
            full = work.tile([P, 2, 256], F32, name="full", bufs=4)
            if h == 0:
                st["F", q, g] = work.tile([P, 4, 256], F32, name="fg", bufs=3)
                st["tb", q, g] = work.tile([P, 4, 256], F32, name="tbg", bufs=3)
                st["ng", q, g] = work.tile([P, 4, 256], F32, name="ngg", bufs=3)
            fg = st["F", q, g]
            for t in range(2):
                k = 4 * g + 2 * h + t
                nc.scalar.activation(out=full[:, t, :], in_=ts[:, t, :], func=AF.Tanh, bias=b1_f[:, k : k + 1])
            pb = work.tile([P, 2, 256], F32, name="pb", bufs=4)
            w = work.tile([P, 2, 256], F32, name="w", bufs=4)
            if i in RATIO:
                sh, scal = r, hb1_f
            else:
                sh, scal = work.tile([P, 2, 256], F32, name="sh", bufs=4), b1_f
                nc.vector.scalar_tensor_tensor(
                    out=sh[:], in0=st["a", i][:], scalar=0.01, in1=r[:], op0=ALU.add, op1=ALU.mult
                )
            for t in range(2):
                k = 4 * g + 2 * h + t
                nc.vector.scalar_tensor_tensor(
                    out=pb[:, t, :], in0=sh[:, t, :], scalar=scal[:, k : k + 1], in1=tu[:, t, :], op0=ALU.mult, op1=ALU.add
                )
            nc.vector.tensor_tensor(out=w[:], in0=pb[:], in1=ts[:], op=ALU.subtract)
            for t in range(2):
                k = 4 * g + 2 * h + t
                nc.vector.tensor_scalar(
                    out=fg[:, 2 * h + t, :], in0=full[:, t, :], scalar1=g_f[:, k : k + 1], scalar2=None, op0=ALU.mult
                )
            st["pb", i], st["w", i] = pb, w

        def tanhs(i):
            q, g, h = idx(i)
            tbg, ngg = st["tb", q, g], st["ng", q, g]
            nb = nhb1_f if i in RATIO else nb1_f
            if i in RATIO:
                for t in range(2):
                    k = 4 * g + 2 * h + t
                    nc.scalar.activation(
                        out=tbg[:, 2 * h + t, :], in_=st["pb", i][:, t, :], func=AF.Tanh, bias=hb1_f[:, k : k + 1]
                    )
            else:
                nc.scalar.activation(out=tbg[:, 2 * h : 2 * h + 2, :], in_=st["pb", i][:], func=AF.Tanh)
            for t in range(2):
                k = 4 * g + 2 * h + t
                nc.scalar.activation(
                    out=ngg[:, 2 * h + t, :], in_=st["w", i][:, t, :], func=AF.Tanh, bias=nb[:, k : k + 1]
                )

        rot = {"d": ["d"], "y": ["y"]}

        def bank_tag(kind):
            tag = rot[kind].pop(0)
            rot[kind].append(tag)
            return tag

        def block(k):
            q, g, m = k // 4, (k // 2) % 2, k % 2
            cols = slice(P * m, P * m + P)
            fg, tbg, ngg = st["F", q, g], st["tb", q, g], st["ng", q, g]
            if k in GP_BLOCKS:
                dn = work.tile([P, 4, P], F32, name="dn", bufs=2)
                dd = work.tile([P, 4, P], F32, name="dd", bufs=2)
                nc.gpsimd.tensor_tensor(out=dn[:], in0=tbg[:, :, cols], in1=ngg[:, :, cols], op=ALU.add)
                nc.gpsimd.tensor_tensor(
                    out=dd[:],
                    in0=dn[:],
                    in1=g_f[:, 4 * g : 4 * g + 4].unsqueeze(2).to_broadcast([P, 4, P]),
                    op=ALU.mult,
                )
            else:
                tag = bank_tag("d")
                dd = psum.tile([P, 4, P], F32, name="dd_" + tag, tag=tag, bufs=2 if tag in ("tu", "ts") else 1)
                for t in range(4):
                    nc.tensor.matmul(dd[:, t, :], lhsT=diag[:, 4 * g + t, :], rhs=tbg[:, t, cols], start=True, stop=False)
                    nc.tensor.matmul(dd[:, t, :], lhsT=diag[:, 4 * g + t, :], rhs=ngg[:, t, cols], start=False, stop=True)
            xy = work.tile([P, 2, P, 4], BF16, name="xy", bufs=4, align_bytes=64)
            dv = dd[:].rearrange("p t (c i) -> p c t i", i=4)
            fv = fg[:, :, cols].rearrange("p t (c i) -> p c t i", i=4)
            nc.vector.tensor_tensor(
                out=xy[:, 0].rearrange("p (c i) t -> p c t i", i=4), in0=fv, in1=dv, op=ALU.add
            )
            nc.vector.tensor_tensor(
                out=xy[:, 1].rearrange("p (c i) t -> p c t i", i=4), in0=fv, in1=dv, op=ALU.subtract
            )
            hc = work.tile([P, 2, P], U32, name="hc", bufs=8, align_bytes=64)
            hs = work.tile([P, 2, P], U8, name="hs", bufs=8, align_bytes=64)
            nc.vector.quantize_mx(
                out=hc[:].rearrange("p s n -> p (s n)").bitcast(FP8X4),
                scales=hs[:].rearrange("p s n -> p (s n)"),
                in_=xy[:].rearrange("p s n t -> p (s n t)"),
            )
            st["h", k] = (hc, hs)

        def second(k, s):
            tag = bank_tag("y")
            yb = psum.tile([P, O], F32, name="y_" + tag, tag=tag, bufs=2 if tag in ("tu", "ts") else 1)
            for g in range(2):
                hc, hs = st["h", k - 2 + 2 * g]
                nc.tensor.matmul_mx(
                    out=yb[:],
                    lhsT=hc[:, s, :].bitcast(FP8X4),
                    lhsT_scale=hs[:, s, :],
                    rhs=w2_t[:, g, :].bitcast(FP4X4),
                    rhs_scale=w2s_t[:, g, :],
                    start=(g == 0),
                    stop=(g == 1),
                )
            st["y", k, s] = yb

        def second_out(k, s):
            q, m = k // 4, k % 2
            yb = st["y", k, s]
            y = work.tile([P, O], F32, name="y", bufs=4)
            if (k, s) in Y_SCALAR:
                nc.scalar.copy(out=y[:], in_=yb[:])
            else:
                nc.vector.tensor_copy(out=y[:], in_=yb[:])
            nc.sync.dma_start(out=outs[s][256 * q + P * m : 256 * q + P * m + P, :], in_=y[:])

        bounds = [sum(CHUNKS[:j]) for j in range(len(CHUNKS) + 1)]
        seen_l, seen_t = set(), set()

        def mm_l(i):
            if i < 16 and i not in seen_l:
                seen_l.add(i)
                magnitudes_mm(i)

        def mm_t(i):
            if i < 16 and i not in seen_t:
                seen_t.add(i)
                split_mm(i)

        xprep(0)
        for i in range(bounds[1]):
            mm_l(i)
            magnitudes(i)
            mm_l(i + 1) if i + 1 < 4 else None
            if i < 3:
                xprep(i + 1)
        todo, ready, late = [], [], []

        def step_block():
            k = todo.pop(0)
            block(k)
            if k % 4 >= 2:
                ready.extend([(k, 0), (k, 1)])

        for j in range(len(CHUNKS)):
            lo, hi = bounds[j], bounds[j + 1]
            last = j == len(CHUNKS) - 1
            if last:
                rot["d"] = ["d", "lb"]
                rot["y"] = ["y", "lg"]
            for i in range(lo, min(hi, lo + LEAD)):
                mm_t(i)
            for i in range(lo, hi):
                log_sum(i)
            nxt = [] if last else list(range(hi, bounds[j + 2]))
            steps = hi - lo + LAG
            done = 0
            for x in range(steps):
                if lo + x < hi:
                    mm_t(lo + x)
                    split(lo + x)
                for i in range(lo + x, min(hi, lo + x + 1 + LEAD)):
                    mm_t(i)
                want = min(len(nxt), -((-(x + 1) * len(nxt)) // max(1, steps - AHEAD)))
                while done < want:
                    mm_l(nxt[done])
                    magnitudes(nxt[done])
                    done += 1
                    if LEAD and done < len(nxt):
                        mm_l(nxt[done])
                i = lo + x - LAG
                if i >= lo:
                    tanhs(i)
                    if i % 2 == 1:
                        todo.extend([i - 1, i])
                while late and late[0][0] <= 0:
                    second_out(*late.pop(0)[1])
                late = [(age - 1, ks) for age, ks in late]
                if todo:
                    step_block()
                for n in range(2 if len(ready) > 2 or not todo else 1):
                    if ready:
                        ks = ready.pop(0)
                        second(*ks)
                        late.append((YDEL if ks in Y_SCALAR else 0, ks))
        while late:
            second_out(*late.pop(0)[1])
        rot["y"] = ["y", "lg", "tu", "ts"]
        rot["d"] = ["d", "lb"]
        while todo or ready:
            while todo:
                step_block()
            while ready:
                ks = ready.pop(0)
                second(*ks)
                second_out(*ks)
